import numpy as np
import ml_dtypes


def mxq(x, axis, fmt="e4m3"):
    dtype, down = {"e4m3": (ml_dtypes.float8_e4m3fn, 7), "e5m2": (ml_dtypes.float8_e5m2, 14)}[fmt]
    v = np.moveaxis(np.asarray(x, np.float32).astype(ml_dtypes.bfloat16).astype(np.float64), axis, -1)
    blocks = v.reshape(v.shape[:-1] + (-1, 32))
    amax = np.abs(blocks).max(-1, keepdims=True)
    byte = np.maximum(np.where(amax > 0, np.frexp(amax)[1] - 1 + 127, 0) - down, 1)
    scale = np.exp2(byte - 127.0)
    codes = (blocks / scale).astype(np.float32).astype(dtype).astype(np.float64)
    return np.moveaxis((codes * scale).reshape(v.shape), -1, axis)


WIDE = False


def mx_kscale(k):
    if not WIDE:
        return np.ones(k)
    levels = np.array([10, -10, 5, -5, 0])
    if k % 512:
        return np.exp2(np.random.permutation(np.resize(levels, k // 32))).repeat(32)
    a = np.empty((k // 512, 16))
    for p in range(k // 512):
        a[p, :8] = np.random.permutation(np.resize(levels, 8))
        for g in range(8):
            far = levels[np.abs(levels - a[p, g]) >= 10]
            a[p, g + 8] = far[np.random.randint(len(far))]
    return np.exp2(a.ravel()).repeat(32)


def f64(x):
    return np.asarray(x).astype(np.float64)


def striped(idx):
    return np.tile(idx.reshape(-1, 16).T, (8, 1)).astype(np.uint16)


def unstriped(offs):
    return offs[:16].T.reshape(-1).astype(np.int64)


E2M1 = np.array([0.0, 0.5, 1.0, 1.5, 2.0, 3.0, 4.0, 6.0, -0.0, -0.5, -1.0, -1.5, -2.0, -3.0, -4.0, -6.0])


def pack_weight(w, fmt):
    k, n = w.shape
    w = f64(np.asarray(w, np.float32).astype(ml_dtypes.bfloat16)).reshape(k // 32, 32, n)
    amax = np.abs(w).max(1)
    if fmt == "e4m3":
        byte = np.frexp(amax)[1] - 1 + 127 - 7
    else:
        mant, ex = np.frexp(amax / 6.0)
        byte = np.where(mant > 0.5, ex, ex - 1) + 127
    byte = np.clip(np.where(amax > 0, byte, 1), 1, 254)
    scaled = (w * np.exp2(127.0 - byte)[:, None, :]).reshape(k, n).astype(np.float32)
    by_word = np.ascontiguousarray(scaled.reshape(k // 512, 128, 4, n).transpose(0, 1, 3, 2))
    if fmt == "e4m3":
        words = by_word.astype(ml_dtypes.float8_e4m3fn).view(np.uint8)
    else:
        c = by_word.astype(ml_dtypes.float4_e2m1fn).view(np.uint8) & 0xF
        words = (c[..., 0::2] | (c[..., 1::2] << 4)).reshape(k // 512, 128, 2 * n)
    return np.ascontiguousarray(words), np.ascontiguousarray(byte.astype(np.uint8).reshape(k // 512, 16, n))


def unpack_weight(words, scales, fmt):
    g, _, n = scales.shape
    words = np.ascontiguousarray(words).reshape(g, 128, n, -1)
    if fmt == "e4m3":
        vals = words.view(ml_dtypes.float8_e4m3fn).astype(np.float64)
    else:
        nib = np.empty((g, 128, n, 4), np.uint8)
        nib[..., 0::2] = words & 0xF
        nib[..., 1::2] = words >> 4
        vals = E2M1[nib]
    vals = vals * np.repeat(np.exp2(scales.astype(np.float64) - 127.0), 8, axis=1)[..., None]
    return vals.transpose(0, 1, 3, 2).reshape(g * 512, n)


def gelu(v):
    return 0.5 * v * (1.0 + np.tanh(np.sqrt(2.0 / np.pi) * (v + 0.044715 * v**3)))


def striped8(idx):
    return np.concatenate([v.reshape(-1, 16).T for v in idx]).astype(np.uint16)


def unstriped8(offs):
    return np.stack([offs[16 * g:16 * g + 16].T.reshape(-1) for g in range(8)]).astype(np.int64)


def heads(h, wgt, idx8):
    r = np.arange(h.shape[0])
    return wgt[r // 4 % 128] * h[r[:, None], idx8[r % 512 // 64]]


def put_heads(h, wgs, idx8, t2):
    r = np.arange(h.shape[0])
    page = np.zeros((h.shape[0], t2))
    page[r[:, None], idx8[r % 512 // 64]] = wgs[r // 4 % 128] * h
    return page


K, T, S, P, H, N, T2 = 512, 4096, 1024, 512, 1024, 1024, 1024

def setup_inputs():
    n = np.random.standard_normal
    s = mx_kscale(K)[:, None]
    u = mx_kscale(H)[:, None]
    d = {}
    d["tab_words"], d["tab_scales"] = pack_weight(n((K, T)) * s, "e4m3")
    d["offs"] = striped(np.random.permutation(T)[:S])
    d["offs2"] = striped8(np.stack([np.random.permutation(S)[:P] for _ in range(8)]))
    d["offs3"] = striped8(np.stack([np.random.permutation(T2)[:P] for _ in range(8)]))
    d["w1"] = (n((K, H)) / s * u.T / K ** 0.5).astype(np.float32)
    d["w2_words"], d["w2_scales"] = pack_weight(n((K, H)) / s / K ** 0.5, "e2m1")
    d["wgt"] = np.repeat(np.random.uniform(0.5, 2.0, (8, P)), 16, axis=0).astype(np.float32)
    d["bt"] = (n(H) * u[:, 0]).astype(np.float32)
    d["w3"] = (n((H, N)) / u / H ** 0.5).astype(np.float32)
    d["w4_words"], d["w4_scales"] = pack_weight(0.7 * n((H, N)) / u / H ** 0.5, "e2m1")
    d["wgo"] = np.repeat(np.random.uniform(0.5, 2.0, (8, P)), 16, axis=0).astype(np.float32)
    return d

def reference(tab_words, tab_scales, offs, offs2, offs3, w1, w2_words, w2_scales,
              wgt, bt, w3, w4_words, w4_scales, wgo):
    v = unpack_weight(tab_words, tab_scales, "e4m3")[:, unstriped(offs)]
    base = mxq(f64(w1), 0, "e4m3").T @ v
    mod = unpack_weight(w2_words, w2_scales, "e2m1").T @ v
    h = base * mod + base
    x = heads(h, f64(wgt), unstriped8(offs2)) + f64(bt)[:, None]
    xq = mxq(x, 0, "e4m3")
    top = mxq(f64(w3), 0, "e4m3").T @ xq
    damp = unpack_weight(w4_words, w4_scales, "e2m1").T @ xq
    y = top / (1.0 + np.abs(damp))
    return put_heads(y, f64(wgo), unstriped8(offs3), T2)

@@ -1,0 +1,205 @@
+from contextlib import ExitStack
+
+import concourse.mybir as mybir
+
+K, T, S, M, H, N, T2 = 512, 4096, 1024, 512, 1024, 1024, 1024
+FLOPS = 2 * (2 * K * H * S + 2 * H * N * M)
+
+F32 = mybir.dt.float32
+BF16 = mybir.dt.bfloat16
+I32 = mybir.dt.int32
+U32 = mybir.dt.uint32
+U16 = mybir.dt.uint16
+U8 = mybir.dt.uint8
+E4M3 = mybir.dt.float8_e4m3fn_x4
+E2M1 = mybir.dt.float4_e2m1fn_x4
+ACT = mybir.ActivationFunctionType
+ALU = mybir.AluOpType
+
+P = 128
+BANK = 512
+PAGES = 4
+
+
+def tile_list_fleece_grade_slots_kernel(tc, tab_words, tab_scales, offs, offs2, offs3, w1, w2_words, w2_scales,
+                                                  wgt, bt, w3, w4_words, w4_scales, wgo, out):
+    nc = tc.nc
+    with ExitStack() as ctx:
+        keep = ctx.enter_context(tc.tile_pool(name="keep", bufs=1))
+        ring = ctx.enter_context(tc.tile_pool(name="ring", bufs=3))
+        psum = ctx.enter_context(tc.psum_pool(name="psum", bufs=4))
+
+        def held(name, shape, dtype):
+            return keep.tile(shape, dtype, name=name, align_bytes=64)
+
+        idx1 = keep.tile([P, S // 16], U16, name="idx1")
+        idx2 = keep.tile([P, M // 16], U16, name="idx2")
+        idx3 = keep.tile([P, M // 16], U16, name="idx3")
+        tabw = held("tabw", [P, T], I32)
+        tabs = held("tabs", [P, T], U8)
+        vw = held("vw", [P, S], U32)
+        vs = held("vs", [P, S], U8)
+        w1_raw = [held("w1_raw%d" % b, [P, 4, 512], F32) for b in range(2)]
+        w1_bf = [held("w1_bf%d" % b, [P, 2048], BF16) for b in range(2)]
+        w1_c = [held("w1_c%d" % b, [P, 512], U32) for b in range(2)]
+        w1_s = [held("w1_s%d" % b, [P, 512], U8) for b in range(2)]
+        w2_raw = held("w2_raw", [P, H // 2], I32)
+        w2_c = held("w2_c", [P, H], U16)
+        w2_sraw = held("w2_sraw", [P, H], U8)
+        w2_s = held("w2_s", [P, H], U8)
+        w3_raw = [[held("w3_raw%d%d" % (b, a), [P, 4, 512], F32) for a in range(2)] for b in range(2)]
+        w3_c = [held("w3_c%d" % u, [P, 512], U32) for u in range(4)]
+        w3_s = [held("w3_s%d" % u, [P, 512], U8) for u in range(4)]
+        w4_raw = held("w4_raw", [P, 2, N // 2], I32)
+        w4_c = held("w4_c", [P, 2 * N], U16)
+        w4_sraw = held("w4_sraw", [P, 2 * N], U8)
+        w4_s = held("w4_s", [P, 2 * N], U8)
+        wgt_sb = held("wgt_sb", [P, M], F32)
+        wgo_sb = held("wgo_sb", [P, M], F32)
+        bt_sb = held("bt_sb", [P, 2, 4], F32)
+        x_pl = [held("x_pl%d" % b, [P, 4, M], BF16) for b in range(2)]
+        x_bf = [held("x_bf%d" % b, [P, 4 * M], BF16) for b in range(2)]
+        x_c = [held("x_c%d" % b, [P, M], U32) for b in range(2)]
+        x_s = [held("x_s%d" % b, [P, M], U8) for b in range(2)]
+        pages = [held("page%d" % u, [P, T2], F32) for u in range(PAGES)]
+
+        nc.vector.memset(tabs[:].bitcast(I32), 0)
+        nc.vector.memset(w2_sraw[:].bitcast(I32), 0)
+        nc.vector.memset(w4_sraw[:].bitcast(I32), 0)
+        for page in pages:
+            nc.vector.memset(page[:], 0.0)
+
+        def load_rows(dst, w, a, b):
+            nc.sync.dma_start(out=dst[:], in_=w[512 * a:512 * (a + 1), 512 * b:512 * (b + 1)].rearrange("(p j) c -> p j c", j=4))
+
+        nc.sync.dma_start(idx1[:], offs)
+        load_rows(w1_raw[0], w1, 0, 0)
+        nc.sync.dma_start(out=tabw[:], in_=tab_words[0].rearrange("p t i -> p (t i)").bitcast(I32))
+        for q in range(4):
+            nc.scalar.dma_start(out=tabs[32 * q:32 * q + 4, :].bitcast(I32), in_=tab_scales[0, 4 * q:4 * q + 4, :].bitcast(I32))
+        nc.scalar.dma_start(out=w2_raw[:], in_=w2_words[0].bitcast(I32))
+        for q in range(4):
+            nc.scalar.dma_start(out=w2_sraw[32 * q:32 * q + 4, :].bitcast(I32), in_=w2_scales[0, 4 * q:4 * q + 4, :].bitcast(I32))
+        nc.sync.dma_start(idx2[:], offs2)
+        nc.sync.dma_start(out=wgt_sb[:], in_=wgt)
+        nc.sync.dma_start(out=bt_sb[:], in_=bt.rearrange("(b p i) -> p b i", b=2, i=4))
+        load_rows(w1_raw[1], w1, 0, 1)
+        for a in range(2):
+            load_rows(w3_raw[0][a], w3, a, 0)
+        nc.sync.dma_start(out=w4_raw[:], in_=w4_words.bitcast(I32).rearrange("a p c -> p a c"))
+        for q in range(4):
+            nc.sync.dma_start(out=w4_sraw[32 * q:32 * q + 4, :].bitcast(I32).rearrange("r (a c) -> r a c", a=2),
+                              in_=w4_scales[:, 4 * q:4 * q + 4, :].bitcast(I32).rearrange("a r c -> r a c"))
+        nc.sync.dma_start(idx3[:], offs3)
+        nc.sync.dma_start(out=wgo_sb[:], in_=wgo)
+        for a in range(2):
+            load_rows(w3_raw[1][a], w3, a, 1)
+
+        def deal(dst, src):
+            nc.vector.tensor_copy(out=dst.rearrange("p (u t m) -> p u t m", t=4, m=P), in_=src.rearrange("p (u m t) -> p u t m", t=4, m=P))
+
+        def w1_round(b, copy):
+            copy(out=w1_bf[b][:].rearrange("p (t m j) -> p m t j", t=4, j=4), in_=w1_raw[b][:].rearrange("p j (m t) -> p m t j", t=4))
+
+        def quantize(codes, scales, src):
+            nc.vector.quantize_mx(out=codes[:].bitcast(E4M3), scales=scales[:], in_=src)
+
+        w1_round(0, nc.vector.tensor_copy)
+        nc.vector.tensor_copy(vs[:], tabs[:].indirect(idx1[:]))
+        quantize(w1_c[0], w1_s[0], w1_bf[0][:])
+        deal(w2_c[:], w2_raw[:].bitcast(U16))
+        deal(w2_s[:], w2_sraw[:])
+        for half in range(2):
+            nc.vector.tensor_copy(vw[:, half * BANK:(half + 1) * BANK], tabw[:].bitcast(U32).indirect(idx1[:, 32 * half:32 * (half + 1)]))
+
+        def features(s, half, h):
+            b, i = divmod(s, 4)
+            cols = slice(half * BANK, (half + 1) * BANK)
+            mod = psum.tile([P, BANK], F32, name="left", tag="left")
+            base = psum.tile([P, BANK], F32, name="right", tag="right")
+            nc.tensor.matmul_mx(out=mod[:], lhsT=w2_c[:, s * P:(s + 1) * P].bitcast(E2M1), lhsT_scale=w2_s[:, s * P:(s + 1) * P],
+                                rhs=vw[:, cols].bitcast(E4M3), rhs_scale=vs[:, cols], start=True, stop=True)
+            nc.tensor.matmul_mx(out=base[:], lhsT=w1_c[b][:, i * P:(i + 1) * P].bitcast(E4M3), lhsT_scale=w1_s[b][:, i * P:(i + 1) * P],
+                                rhs=vw[:, cols].bitcast(E4M3), rhs_scale=vs[:, cols], start=True, stop=True)
+            mod_sb = ring.tile([P, BANK], F32, name="mod_sb")
+            nc.scalar.copy(out=mod_sb[:], in_=mod[:])
+            nc.vector.scalar_tensor_tensor(out=h[:, cols], in0=mod_sb[:], scalar=1.0, in1=base[:], op0=ALU.add, op1=ALU.mult)
+
+        def pick(s, h):
+            b, i = divmod(s, 4)
+            picked = ring.tile([P, M], F32, name="picked")
+            nc.vector.tensor_tensor(picked[:], h[:].indirect(idx2[:]), wgt_sb[:], ALU.mult)
+            nc.scalar.activation(out=x_pl[b][:, i, :], in_=picked[:], func=ACT.Identity, bias=bt_sb[:, b, i:i + 1])
+
+        def x_weave(b, copy):
+            copy(out=x_bf[b][:].rearrange("p (c e i) -> p c i e", e=4, i=4), in_=x_pl[b][:].rearrange("p i (c e) -> p c i e", e=4))
+
+        def w3_prepare(u):
+            b, pair = divmod(u, 2)
+            w3_bf = ring.tile([P, 2, 1024], BF16, name="w3_bf", align_bytes=64)
+            for a in range(2):
+                nc.scalar.copy(out=w3_bf[:, a, :].rearrange("p (t m j) -> p m t j", t=2, j=4),
+                               in_=w3_raw[b][a][:].rearrange("p j (m t) -> p m t j", t=4)[:, :, 2 * pair:2 * pair + 2, :])
+            quantize(w3_c[u], w3_s[u], w3_bf[:].rearrange("p a c -> p (a c)"))
+
+        hs = []
+        for s in range(8):
+            h = ring.tile([P, S], F32, name="h")
+            hs.append(h)
+            features(s, 0, h)
+            if s > 0:
+                pick(s - 1, hs[s - 1])
+            features(s, 1, h)
+            if s == 1:
+                w1_round(1, nc.scalar.copy)
+            if s == 2:
+                quantize(w1_c[1], w1_s[1], w1_bf[1][:])
+            if s == 4:
+                x_weave(0, nc.scalar.copy)
+            if s == 5:
+                quantize(x_c[0], x_s[0], x_bf[0][:])
+                deal(w4_c[:], w4_raw[:].rearrange("p a c -> p (a c)").bitcast(U16))
+                deal(w4_s[:], w4_sraw[:])
+            if s == 6:
+                w3_prepare(0)
+        pick(7, hs[7])
+        x_weave(1, nc.vector.tensor_copy)
+        quantize(x_c[1], x_s[1], x_bf[1][:])
+
+        def grade(s):
+            b, i = divmod(s, 4)
+            u, t = divmod(s, 2)
+            damp = psum.tile([P, BANK], F32, name="left", tag="left")
+            top = psum.tile([P, BANK], F32, name="right", tag="right")
+            for a in range(2):
+                cols = slice(a * N + s * P, a * N + (s + 1) * P)
+                nc.tensor.matmul_mx(out=damp[:], lhsT=w4_c[:, cols].bitcast(E2M1), lhsT_scale=w4_s[:, cols],
+                                    rhs=x_c[a][:].bitcast(E4M3), rhs_scale=x_s[a][:], start=(a == 0), stop=(a == 1))
+            for a in range(2):
+                cols = slice((2 * a + t) * P, (2 * a + t + 1) * P)
+                nc.tensor.matmul_mx(out=top[:], lhsT=w3_c[u][:, cols].bitcast(E4M3), lhsT_scale=w3_s[u][:, cols],
+                                    rhs=x_c[a][:].bitcast(E4M3), rhs_scale=x_s[a][:], start=(a == 0), stop=(a == 1))
+            size = ring.tile([P, M], F32, name="size")
+            nc.scalar.activation(out=size[:], in_=damp[:], func=ACT.Abs)
+            root = ring.tile([P, M], F32, name="root")
+            nc.scalar.activation(out=root[:], in_=size[:], func=ACT.Abs_reciprocal_sqrt, bias=1.0)
+            inv = ring.tile([P, M], F32, name="inv")
+            nc.scalar.activation(out=inv[:], in_=root[:], func=ACT.Square)
+            y = ring.tile([P, M], F32, name="y")
+            nc.vector.tensor_tensor(y[:], top[:], inv[:], ALU.mult)
+            return y
+
+        def enter(s, y):
+            b, i = divmod(s, 4)
+            page = pages[s % PAGES]
+            nc.vector.tensor_tensor(page[:].indirect(idx3[:]), y[:], wgo_sb[:], ALU.mult)
+            nc.sync.dma_start(out=out[512 * b:512 * (b + 1), :].rearrange("(p i) c -> p i c", i=4)[:, i, :], in_=page[:])
+
+        ys = []
+        for s in range(8):
+            ys.append(grade(s))
+            if s % 2 == 0 and s < 6:
+                w3_prepare(s // 2 + 1)
+            if s > 0:
+                enter(s - 1, ys[s - 1])
+        enter(7, ys[7])

@@ -18,7 +18,8 @@ ALU = mybir.AluOpType
 
 P = 128
 BANK = 512
-PAGES = 4
+MH = M // 2
+SPLIT = 3
 
 
 def tile_list_fleece_grade_slots_kernel(tc, tab_words, tab_scales, offs, offs2, offs3, w1, w2_words, w2_scales,
@@ -29,25 +30,26 @@ def tile_list_fleece_grade_slots_kernel(tc, tab_words, tab_scales, offs, offs2, 
         ring = ctx.enter_context(tc.tile_pool(name="ring", bufs=3))
         psum = ctx.enter_context(tc.psum_pool(name="psum", bufs=4))
 
-        def held(name, shape, dtype):
-            return keep.tile(shape, dtype, name=name, align_bytes=64)
+        def held(name, shape, dtype, tag=None):
+            return keep.tile(shape, dtype, name=name, tag=tag or name, align_bytes=64)
 
         idx1 = keep.tile([P, S // 16], U16, name="idx1")
         idx2 = keep.tile([P, M // 16], U16, name="idx2")
         idx3 = keep.tile([P, M // 16], U16, name="idx3")
         tabw = held("tabw", [P, T], I32)
         tabs = held("tabs", [P, T], U8)
+        w2_rows = held("w2_rows", [P, H // 4], I32)
         vw = held("vw", [P, S], U32)
         vs = held("vs", [P, S], U8)
-        w1_raw = [held("w1_raw%d" % b, [P, 4, 512], F32) for b in range(2)]
-        w1_bf = [held("w1_bf%d" % b, [P, 2048], BF16) for b in range(2)]
+        w1_raw0 = [held("w1_raw0%d" % c, [P, 4, 256], F32) for c in range(2)]
+        w1_raw1 = held("w1_raw1", [P, 4, 512], F32, "raw_a")
+        w1_bf = [held("w1_bf0", [P, 2048], BF16)]
         w1_c = [held("w1_c%d" % b, [P, 512], U32) for b in range(2)]
         w1_s = [held("w1_s%d" % b, [P, 512], U8) for b in range(2)]
         w2_raw = held("w2_raw", [P, H // 2], I32)
         w2_c = held("w2_c", [P, H], U16)
         w2_sraw = held("w2_sraw", [P, H], U8)
         w2_s = held("w2_s", [P, H], U8)
-        w3_raw = [[held("w3_raw%d%d" % (b, a), [P, 4, 512], F32) for a in range(2)] for b in range(2)]
         w3_c = [held("w3_c%d" % u, [P, 512], U32) for u in range(4)]
         w3_s = [held("w3_s%d" % u, [P, 512], U8) for u in range(4)]
         w4_raw = held("w4_raw", [P, 2, N // 2], I32)
@@ -57,62 +59,69 @@ def tile_list_fleece_grade_slots_kernel(tc, tab_words, tab_scales, offs, offs2, 
         wgt_sb = held("wgt_sb", [P, M], F32)
         wgo_sb = held("wgo_sb", [P, M], F32)
         bt_sb = held("bt_sb", [P, 2, 4], F32)
-        x_pl = [held("x_pl%d" % b, [P, 4, M], BF16) for b in range(2)]
-        x_bf = [held("x_bf%d" % b, [P, 4 * M], BF16) for b in range(2)]
+        x_pl = [[held("x_pl%d%d" % (f, b), [P, 4, MH], BF16) for b in range(2)] for f in range(2)]
         x_c = [held("x_c%d" % b, [P, M], U32) for b in range(2)]
         x_s = [held("x_s%d" % b, [P, M], U8) for b in range(2)]
-        pages = [held("page%d" % u, [P, T2], F32) for u in range(PAGES)]
+        hs = [held("h%d" % s, [P, S], F32) for s in range(8)]
+        pages = [held("page%d" % s, [P, T2], F32) for s in range(8)]
 
         nc.vector.memset(tabs[:].bitcast(I32), 0)
         nc.vector.memset(w2_sraw[:].bitcast(I32), 0)
-        nc.vector.memset(w4_sraw[:].bitcast(I32), 0)
-        for page in pages:
-            nc.vector.memset(page[:], 0.0)
+        nc.gpsimd.memset(w4_sraw[:].bitcast(I32), 0)
+        for s in range(8):
+            if s < 4:
+                nc.vector.memset(pages[s][:], 0.0)
+            else:
+                nc.gpsimd.memset(pages[s][:], 0.0)
 
-        def load_rows(dst, w, a, b):
-            nc.sync.dma_start(out=dst[:], in_=w[512 * a:512 * (a + 1), 512 * b:512 * (b + 1)].rearrange("(p j) c -> p j c", j=4))
+        def load_rows(dst, w, a, c0, c1):
+            nc.sync.dma_start(out=dst[:], in_=w[512 * a:512 * (a + 1), c0:c1].rearrange("(p j) c -> p j c", j=4))
 
         nc.sync.dma_start(idx1[:], offs)
-        load_rows(w1_raw[0], w1, 0, 0)
+        for q in range(4):
+            nc.sync.dma_start(out=w2_rows[32 * q:32 * q + 4, :], in_=w2_scales[0, 4 * q:4 * q + 4, :].bitcast(I32))
         nc.sync.dma_start(out=tabw[:], in_=tab_words[0].rearrange("p t i -> p (t i)").bitcast(I32))
+        nc.sync.dma_start(out=w2_raw[:], in_=w2_words[0].bitcast(I32))
+        load_rows(w1_raw0[0], w1, 0, 0, 256)
+        load_rows(w1_raw0[1], w1, 0, 256, 512)
         for q in range(4):
             nc.scalar.dma_start(out=tabs[32 * q:32 * q + 4, :].bitcast(I32), in_=tab_scales[0, 4 * q:4 * q + 4, :].bitcast(I32))
-        nc.scalar.dma_start(out=w2_raw[:], in_=w2_words[0].bitcast(I32))
-        for q in range(4):
-            nc.scalar.dma_start(out=w2_sraw[32 * q:32 * q + 4, :].bitcast(I32), in_=w2_scales[0, 4 * q:4 * q + 4, :].bitcast(I32))
         nc.sync.dma_start(idx2[:], offs2)
         nc.sync.dma_start(out=wgt_sb[:], in_=wgt)
         nc.sync.dma_start(out=bt_sb[:], in_=bt.rearrange("(b p i) -> p b i", b=2, i=4))
-        load_rows(w1_raw[1], w1, 0, 1)
+        load_rows(w1_raw1, w1, 0, 512, 1024)
+        w3_raw = [[held("w3_raw0%d" % a, [P, 4, 512], F32) for a in range(2)]]
         for a in range(2):
-            load_rows(w3_raw[0][a], w3, a, 0)
+            load_rows(w3_raw[0][a], w3, a, 0, 512)
         nc.sync.dma_start(out=w4_raw[:], in_=w4_words.bitcast(I32).rearrange("a p c -> p a c"))
         for q in range(4):
             nc.sync.dma_start(out=w4_sraw[32 * q:32 * q + 4, :].bitcast(I32).rearrange("r (a c) -> r a c", a=2),
                               in_=w4_scales[:, 4 * q:4 * q + 4, :].bitcast(I32).rearrange("a r c -> r a c"))
         nc.sync.dma_start(idx3[:], offs3)
         nc.sync.dma_start(out=wgo_sb[:], in_=wgo)
-        for a in range(2):
-            load_rows(w3_raw[1][a], w3, a, 1)
 
-        def deal(dst, src):
-            nc.vector.tensor_copy(out=dst.rearrange("p (u t m) -> p u t m", t=4, m=P), in_=src.rearrange("p (u m t) -> p u t m", t=4, m=P))
+        def deal(copy, dst, src):
+            copy(out=dst.rearrange("p (u t m) -> p u t m", t=4, m=P), in_=src.rearrange("p (u m t) -> p u t m", t=4, m=P))
 
-        def w1_round(b, copy):
-            copy(out=w1_bf[b][:].rearrange("p (t m j) -> p m t j", t=4, j=4), in_=w1_raw[b][:].rearrange("p j (m t) -> p m t j", t=4))
+        def w1_round(copy, b, raw, m0):
+            n = raw.shape[2] // 4
+            copy(out=w1_bf[b][:].rearrange("p (t m j) -> p m t j", t=4, j=4)[:, m0:m0 + n], in_=raw[:].rearrange("p j (m t) -> p m t j", t=4))
 
         def quantize(codes, scales, src):
-            nc.vector.quantize_mx(out=codes[:].bitcast(E4M3), scales=scales[:], in_=src)
+            nc.vector.quantize_mx(out=codes.bitcast(E4M3), scales=scales, in_=src)
 
-        w1_round(0, nc.vector.tensor_copy)
+        for q in range(4):
+            nc.vector.tensor_copy(out=w2_sraw[32 * q:32 * q + 4, :].bitcast(I32), in_=w2_rows[32 * q:32 * q + 4, :])
+        deal(nc.vector.tensor_copy, w2_s[:], w2_sraw[:])
         nc.vector.tensor_copy(vs[:], tabs[:].indirect(idx1[:]))
-        quantize(w1_c[0], w1_s[0], w1_bf[0][:])
-        deal(w2_c[:], w2_raw[:].bitcast(U16))
-        deal(w2_s[:], w2_sraw[:])
         for half in range(2):
             nc.vector.tensor_copy(vw[:, half * BANK:(half + 1) * BANK], tabw[:].bitcast(U32).indirect(idx1[:, 32 * half:32 * (half + 1)]))
+        deal(nc.scalar.copy, w2_c[:], w2_raw[:].bitcast(U16))
+        w1_round(nc.scalar.copy, 0, w1_raw0[0], 0)
+        w1_round(nc.vector.tensor_copy, 0, w1_raw0[1], 64)
+        quantize(w1_c[0][:], w1_s[0][:], w1_bf[0][:])
 
-        def features(s, half, h):
+        def features(s, half, mod_sb):
             b, i = divmod(s, 4)
             cols = slice(half * BANK, (half + 1) * BANK)
             mod = psum.tile([P, BANK], F32, name="left", tag="left")
@@ -121,85 +130,108 @@ def tile_list_fleece_grade_slots_kernel(tc, tab_words, tab_scales, offs, offs2, 
                                 rhs=vw[:, cols].bitcast(E4M3), rhs_scale=vs[:, cols], start=True, stop=True)
             nc.tensor.matmul_mx(out=base[:], lhsT=w1_c[b][:, i * P:(i + 1) * P].bitcast(E4M3), lhsT_scale=w1_s[b][:, i * P:(i + 1) * P],
                                 rhs=vw[:, cols].bitcast(E4M3), rhs_scale=vs[:, cols], start=True, stop=True)
-            mod_sb = ring.tile([P, BANK], F32, name="mod_sb")
             nc.scalar.copy(out=mod_sb[:], in_=mod[:])
-            nc.vector.scalar_tensor_tensor(out=h[:, cols], in0=mod_sb[:], scalar=1.0, in1=base[:], op0=ALU.add, op1=ALU.mult)
+            nc.vector.scalar_tensor_tensor(out=hs[s][:, cols], in0=mod_sb[:], scalar=1.0, in1=base[:], op0=ALU.add, op1=ALU.mult)
 
-        def pick(s, h):
+        def pick(s, f, picked):
             b, i = divmod(s, 4)
-            picked = ring.tile([P, M], F32, name="picked")
-            nc.vector.tensor_tensor(picked[:], h[:].indirect(idx2[:]), wgt_sb[:], ALU.mult)
-            nc.scalar.activation(out=x_pl[b][:, i, :], in_=picked[:], func=ACT.Identity, bias=bt_sb[:, b, i:i + 1])
+            window = hs[s][:].indirect(idx2[:, 16 * f:16 * (f + 1)])
+            weights = wgt_sb[:, f * MH:(f + 1) * MH]
+            nc.vector.tensor_tensor(picked, window, weights, ALU.mult)
+            nc.scalar.activation(out=x_pl[f][b][:, i, :], in_=picked, func=ACT.Identity, bias=bt_sb[:, b, i:i + 1])
 
-        def x_weave(b, copy):
-            copy(out=x_bf[b][:].rearrange("p (c e i) -> p c i e", e=4, i=4), in_=x_pl[b][:].rearrange("p i (c e) -> p c i e", e=4))
+        def x_quantize(copy, f, b):
+            x_bf = ring.tile([P, 4 * MH], BF16, name="x_bf", align_bytes=64)
+            copy(out=x_bf[:].rearrange("p (c e i) -> p c i e", e=4, i=4), in_=x_pl[f][b][:].rearrange("p i (c e) -> p c i e", e=4))
+            quantize(x_c[b][:, f * MH:(f + 1) * MH], x_s[b][:, f * MH:(f + 1) * MH], x_bf[:])
+
+        def w4_deal(b):
+            words = w4_raw[:].bitcast(U16).rearrange("p a (b m t) -> p a b t m", b=2, t=4)[:, :, b]
+            nc.scalar.copy(out=w4_c[:].rearrange("p (b a t m) -> p b a t m", b=2, a=2, t=4)[:, b], in_=words)
+            nc.vector.tensor_copy(out=w4_s[:].rearrange("p (b a t m) -> p b a t m", b=2, a=2, t=4)[:, b],
+                                  in_=w4_sraw[:].rearrange("p (a b m t) -> p a b t m", a=2, b=2, t=4)[:, :, b])
 
         def w3_prepare(u):
             b, pair = divmod(u, 2)
-            w3_bf = ring.tile([P, 2, 1024], BF16, name="w3_bf", align_bytes=64)
+            w3_bf = ring.tile([P, 2, 1024], BF16, name="w3_bf", align_bytes=64, bufs=2)
             for a in range(2):
                 nc.scalar.copy(out=w3_bf[:, a, :].rearrange("p (t m j) -> p m t j", t=2, j=4),
                                in_=w3_raw[b][a][:].rearrange("p j (m t) -> p m t j", t=4)[:, :, 2 * pair:2 * pair + 2, :])
-            quantize(w3_c[u], w3_s[u], w3_bf[:].rearrange("p a c -> p (a c)"))
+            quantize(w3_c[u][:], w3_s[u][:], w3_bf[:].rearrange("p a c -> p (a c)"))
 
-        hs = []
         for s in range(8):
-            h = ring.tile([P, S], F32, name="h")
-            hs.append(h)
-            features(s, 0, h)
+            if s == 0:
+                features(s, 0, held("mod_first", [P, BANK], F32, "first"))
+            else:
+                features(s, 0, ring.tile([P, BANK], F32, name="mod_sb"))
             if s > 0:
-                pick(s - 1, hs[s - 1])
-            features(s, 1, h)
-            if s == 1:
-                w1_round(1, nc.scalar.copy)
+                pick(s - 1, 0, ring.tile([P, MH], F32, name="picked")[:])
+            if s < 7:
+                features(s, 1, ring.tile([P, BANK], F32, name="mod_sb"))
+            else:
+                features(s, 1, held("mod_last", [P, BANK], F32, "late"))
+            if s == 0:
+                w1_bf.append(held("w1_bf1", [P, 2048], BF16, "first"))
+                w1_round(nc.scalar.copy, 1, w1_raw1, 0)
             if s == 2:
-                quantize(w1_c[1], w1_s[1], w1_bf[1][:])
-            if s == 4:
-                x_weave(0, nc.scalar.copy)
-            if s == 5:
-                quantize(x_c[0], x_s[0], x_bf[0][:])
-                deal(w4_c[:], w4_raw[:].rearrange("p a c -> p (a c)").bitcast(U16))
-                deal(w4_s[:], w4_sraw[:])
-            if s == 6:
+                quantize(w1_c[1][:], w1_s[1][:], w1_bf[1][:])
+                w3_raw.append([held("w3_raw10", [P, 4, 512], F32, "raw_a"), held("w3_raw11", [P, 4, 512], F32, "tabw")])
+                for a in range(2):
+                    load_rows(w3_raw[1][a], w3, a, 512, 1024)
+            if s == 3:
                 w3_prepare(0)
-        pick(7, hs[7])
-        x_weave(1, nc.vector.tensor_copy)
-        quantize(x_c[1], x_s[1], x_bf[1][:])
+            if s == 4:
+                x_quantize(nc.scalar.copy, 0, 0)
+            if s == 6:
+                w4_deal(0)
+        pick(7, 0, ring.tile([P, MH], F32, name="picked")[:])
+        x_quantize(nc.scalar.copy, 0, 1)
 
-        def grade(s):
+        def grade(s, m0, m1):
             b, i = divmod(s, 4)
             u, t = divmod(s, 2)
-            damp = psum.tile([P, BANK], F32, name="left", tag="left")
-            top = psum.tile([P, BANK], F32, name="right", tag="right")
+            damp = psum.tile([P, m1 - m0], F32, name="left", tag="left")
+            top = psum.tile([P, m1 - m0], F32, name="right", tag="right")
             for a in range(2):
-                cols = slice(a * N + s * P, a * N + (s + 1) * P)
+                cols = slice((8 * b + 4 * a + i) * P, (8 * b + 4 * a + i + 1) * P)
                 nc.tensor.matmul_mx(out=damp[:], lhsT=w4_c[:, cols].bitcast(E2M1), lhsT_scale=w4_s[:, cols],
-                                    rhs=x_c[a][:].bitcast(E4M3), rhs_scale=x_s[a][:], start=(a == 0), stop=(a == 1))
+                                    rhs=x_c[a][:, m0:m1].bitcast(E4M3), rhs_scale=x_s[a][:, m0:m1], start=(a == 0), stop=(a == 1))
             for a in range(2):
                 cols = slice((2 * a + t) * P, (2 * a + t + 1) * P)
                 nc.tensor.matmul_mx(out=top[:], lhsT=w3_c[u][:, cols].bitcast(E4M3), lhsT_scale=w3_s[u][:, cols],
-                                    rhs=x_c[a][:].bitcast(E4M3), rhs_scale=x_s[a][:], start=(a == 0), stop=(a == 1))
-            size = ring.tile([P, M], F32, name="size")
+                                    rhs=x_c[a][:, m0:m1].bitcast(E4M3), rhs_scale=x_s[a][:, m0:m1], start=(a == 0), stop=(a == 1))
+            size = ring.tile([P, m1 - m0], F32, name="size")
             nc.scalar.activation(out=size[:], in_=damp[:], func=ACT.Abs)
-            root = ring.tile([P, M], F32, name="root")
+            root = ring.tile([P, m1 - m0], F32, name="root")
             nc.scalar.activation(out=root[:], in_=size[:], func=ACT.Abs_reciprocal_sqrt, bias=1.0)
-            inv = ring.tile([P, M], F32, name="inv")
+            inv = ring.tile([P, m1 - m0], F32, name="inv")
             nc.scalar.activation(out=inv[:], in_=root[:], func=ACT.Square)
-            y = ring.tile([P, M], F32, name="y")
+            y = ring.tile([P, m1 - m0], F32, name="y")
             nc.vector.tensor_tensor(y[:], top[:], inv[:], ALU.mult)
             return y
 
-        def enter(s, y):
+        def enter(s, m0, m1, y):
             b, i = divmod(s, 4)
-            page = pages[s % PAGES]
-            nc.vector.tensor_tensor(page[:].indirect(idx3[:]), y[:], wgo_sb[:], ALU.mult)
-            nc.sync.dma_start(out=out[512 * b:512 * (b + 1), :].rearrange("(p i) c -> p i c", i=4)[:, i, :], in_=page[:])
+            nc.vector.tensor_tensor(pages[s][:].indirect(idx3[:, m0 // 16:m1 // 16]), y[:], wgo_sb[:, m0:m1], ALU.mult)
+            if m1 == M:
+                nc.sync.dma_start(out=out[512 * b:512 * (b + 1), :].rearrange("(p i) c -> p i c", i=4)[:, i, :], in_=pages[s][:])
 
-        ys = []
+        late = held("late", [P, 8, MH], F32, "late")
+        units = [(s, 0, MH) for s in range(SPLIT)] + [(s, MH, M) for s in range(SPLIT)] + [(s, 0, M) for s in range(SPLIT, 8)]
+        ys = [grade(*units[0])]
         for s in range(8):
-            ys.append(grade(s))
-            if s % 2 == 0 and s < 6:
-                w3_prepare(s // 2 + 1)
-            if s > 0:
-                enter(s - 1, ys[s - 1])
-        enter(7, ys[7])
+            pick(s, 1, late[:, s, :])
+            if s == 3:
+                x_quantize(nc.scalar.copy, 1, 0)
+        w3_prepare(1)
+        x_quantize(nc.scalar.copy, 1, 1)
+        for n in range(1, len(units)):
+            ys.append(grade(*units[n]))
+            if n == 2:
+                w4_deal(1)
+            if n == 3:
+                w3_prepare(2)
+            if n == 6:
+                w3_prepare(3)
+            enter(*units[n - 1], ys[n - 1])
+        enter(*units[-1], ys[-1])

@@ -207,12 +207,12 @@ def tile_list_fleece_grade_slots_kernel(tc, tab_words, tab_scales, offs, offs2, 
             inv = ring.tile([P, m1 - m0], F32, name="inv")
             nc.scalar.activation(out=inv[:], in_=root[:], func=ACT.Square)
             y = ring.tile([P, m1 - m0], F32, name="y")
-            nc.vector.tensor_tensor(y[:], top[:], inv[:], ALU.mult)
-            return y
+            nc.vector.tensor_tensor(y[:], top[:], wgo_sb[:, m0:m1], ALU.mult)
+            return y, inv
 
-        def enter(s, m0, m1, y):
+        def enter(s, m0, m1, y, inv):
             b, i = divmod(s, 4)
-            nc.vector.tensor_tensor(pages[s][:].indirect(idx3[:, m0 // 16:m1 // 16]), y[:], wgo_sb[:, m0:m1], ALU.mult)
+            nc.vector.tensor_tensor(pages[s][:].indirect(idx3[:, m0 // 16:m1 // 16]), y[:], inv[:], ALU.mult)
             if m1 == M:
                 nc.sync.dma_start(out=out[512 * b:512 * (b + 1), :].rearrange("(p i) c -> p i c", i=4)[:, i, :], in_=pages[s][:])
 
@@ -233,5 +233,5 @@ def tile_list_fleece_grade_slots_kernel(tc, tab_words, tab_scales, offs, offs2, 
                 w3_prepare(2)
             if n == 6:
                 w3_prepare(3)
-            enter(*units[n - 1], ys[n - 1])
-        enter(*units[-1], ys[-1])
+            enter(*units[n - 1], *ys[n - 1])
+        enter(*units[-1], *ys[-1])

@@ -20,6 +20,7 @@ P = 128
 BANK = 512
 MH = M // 2
 SPLIT = 3
+PAGES = 4
 
 
 def tile_list_fleece_grade_slots_kernel(tc, tab_words, tab_scales, offs, offs2, offs3, w1, w2_words, w2_scales,
@@ -63,16 +64,13 @@ def tile_list_fleece_grade_slots_kernel(tc, tab_words, tab_scales, offs, offs2, 
         x_c = [held("x_c%d" % b, [P, M], U32) for b in range(2)]
         x_s = [held("x_s%d" % b, [P, M], U8) for b in range(2)]
         hs = [held("h%d" % s, [P, S], F32) for s in range(8)]
-        pages = [held("page%d" % s, [P, T2], F32) for s in range(8)]
+        pages = [held("page%d" % s, [P, T2], F32) for s in range(PAGES)]
 
         nc.vector.memset(tabs[:].bitcast(I32), 0)
         nc.vector.memset(w2_sraw[:].bitcast(I32), 0)
-        nc.gpsimd.memset(w4_sraw[:].bitcast(I32), 0)
-        for s in range(8):
-            if s < 4:
-                nc.vector.memset(pages[s][:], 0.0)
-            else:
-                nc.gpsimd.memset(pages[s][:], 0.0)
+        nc.vector.memset(w4_sraw[:].bitcast(I32), 0)
+        for page in pages:
+            nc.vector.memset(page[:], 0.0)
 
         def load_rows(dst, w, a, c0, c1):
             nc.sync.dma_start(out=dst[:], in_=w[512 * a:512 * (a + 1), c0:c1].rearrange("(p j) c -> p j c", j=4))
@@ -212,9 +210,9 @@ def tile_list_fleece_grade_slots_kernel(tc, tab_words, tab_scales, offs, offs2, 
 
         def enter(s, m0, m1, y, inv):
             b, i = divmod(s, 4)
-            nc.vector.tensor_tensor(pages[s][:].indirect(idx3[:, m0 // 16:m1 // 16]), y[:], inv[:], ALU.mult)
+            nc.vector.tensor_tensor(pages[s % PAGES][:].indirect(idx3[:, m0 // 16:m1 // 16]), y[:], inv[:], ALU.mult)
             if m1 == M:
-                nc.sync.dma_start(out=out[512 * b:512 * (b + 1), :].rearrange("(p i) c -> p i c", i=4)[:, i, :], in_=pages[s][:])
+                nc.sync.dma_start(out=out[512 * b:512 * (b + 1), :].rearrange("(p i) c -> p i c", i=4)[:, i, :], in_=pages[s % PAGES][:])
 
         late = held("late", [P, 8, MH], F32, "late")
         units = [(s, 0, MH) for s in range(SPLIT)] + [(s, MH, M) for s in range(SPLIT)] + [(s, 0, M) for s in range(SPLIT, 8)]

from contextlib import ExitStack

import concourse.mybir as mybir

K, T, S, M, H, N, T2 = 512, 4096, 1024, 512, 1024, 1024, 1024
FLOPS = 2 * (2 * K * H * S + 2 * H * N * M)

F32 = mybir.dt.float32
BF16 = mybir.dt.bfloat16
I32 = mybir.dt.int32
U32 = mybir.dt.uint32
U16 = mybir.dt.uint16
U8 = mybir.dt.uint8
E4M3 = mybir.dt.float8_e4m3fn_x4
E2M1 = mybir.dt.float4_e2m1fn_x4
ACT = mybir.ActivationFunctionType
ALU = mybir.AluOpType

P = 128
BANK = 512
MH = M // 2
SPLIT = 3
PAGES = 4


def tile_list_fleece_grade_slots_kernel(tc, tab_words, tab_scales, offs, offs2, offs3, w1, w2_words, w2_scales,
                                                  wgt, bt, w3, w4_words, w4_scales, wgo, out):
    nc = tc.nc
    with ExitStack() as ctx:
        keep = ctx.enter_context(tc.tile_pool(name="keep", bufs=1))
        ring = ctx.enter_context(tc.tile_pool(name="ring", bufs=3))
        psum = ctx.enter_context(tc.psum_pool(name="psum", bufs=4))

        def held(name, shape, dtype, tag=None):
            return keep.tile(shape, dtype, name=name, tag=tag or name, align_bytes=64)

        idx1 = keep.tile([P, S // 16], U16, name="idx1")
        idx2 = keep.tile([P, M // 16], U16, name="idx2")
        idx3 = keep.tile([P, M // 16], U16, name="idx3")
        tabw = held("tabw", [P, T], I32)
        tabs = held("tabs", [P, T], U8)
        w2_rows = held("w2_rows", [P, H // 4], I32)
        vw = held("vw", [P, S], U32)
        vs = held("vs", [P, S], U8)
        w1_raw0 = [held("w1_raw0%d" % c, [P, 4, 256], F32) for c in range(2)]
        w1_raw1 = held("w1_raw1", [P, 4, 512], F32, "raw_a")
        w1_bf = [held("w1_bf0", [P, 2048], BF16)]
        w1_c = [held("w1_c%d" % b, [P, 512], U32) for b in range(2)]
        w1_s = [held("w1_s%d" % b, [P, 512], U8) for b in range(2)]
        w2_raw = held("w2_raw", [P, H // 2], I32)
        w2_c = held("w2_c", [P, H], U16)
        w2_sraw = held("w2_sraw", [P, H], U8)
        w2_s = held("w2_s", [P, H], U8)
        w3_c = [held("w3_c%d" % u, [P, 512], U32) for u in range(4)]
        w3_s = [held("w3_s%d" % u, [P, 512], U8) for u in range(4)]
        w4_raw = held("w4_raw", [P, 2, N // 2], I32)
        w4_c = held("w4_c", [P, 2 * N], U16)
        w4_sraw = held("w4_sraw", [P, 2 * N], U8)
        w4_s = held("w4_s", [P, 2 * N], U8)
        wgt_sb = held("wgt_sb", [P, M], F32)
        wgo_sb = held("wgo_sb", [P, M], F32)
        bt_sb = held("bt_sb", [P, 2, 4], F32)
        x_pl = [[held("x_pl%d%d" % (f, b), [P, 4, MH], BF16) for b in range(2)] for f in range(2)]
        x_c = [held("x_c%d" % b, [P, M], U32) for b in range(2)]
        x_s = [held("x_s%d" % b, [P, M], U8) for b in range(2)]
        hs = [held("h%d" % s, [P, S], F32) for s in range(8)]
        pages = [held("page%d" % s, [P, T2], F32) for s in range(PAGES)]

        nc.vector.memset(tabs[:].bitcast(I32), 0)
        nc.vector.memset(w2_sraw[:].bitcast(I32), 0)
        nc.vector.memset(w4_sraw[:].bitcast(I32), 0)
        for page in pages:
            nc.vector.memset(page[:], 0.0)

        def load_rows(dst, w, a, c0, c1):
            nc.sync.dma_start(out=dst[:], in_=w[512 * a:512 * (a + 1), c0:c1].rearrange("(p j) c -> p j c", j=4))

        nc.sync.dma_start(idx1[:], offs)
        for q in range(4):
            nc.sync.dma_start(out=w2_rows[32 * q:32 * q + 4, :], in_=w2_scales[0, 4 * q:4 * q + 4, :].bitcast(I32))
        nc.sync.dma_start(out=tabw[:], in_=tab_words[0].rearrange("p t i -> p (t i)").bitcast(I32))
        nc.sync.dma_start(out=w2_raw[:], in_=w2_words[0].bitcast(I32))
        load_rows(w1_raw0[0], w1, 0, 0, 256)
        load_rows(w1_raw0[1], w1, 0, 256, 512)
        for q in range(4):
            nc.scalar.dma_start(out=tabs[32 * q:32 * q + 4, :].bitcast(I32), in_=tab_scales[0, 4 * q:4 * q + 4, :].bitcast(I32))
        nc.sync.dma_start(idx2[:], offs2)
        nc.sync.dma_start(out=wgt_sb[:], in_=wgt)
        nc.sync.dma_start(out=bt_sb[:], in_=bt.rearrange("(b p i) -> p b i", b=2, i=4))
        load_rows(w1_raw1, w1, 0, 512, 1024)
        w3_raw = [[held("w3_raw0%d" % a, [P, 4, 512], F32) for a in range(2)]]
        for a in range(2):
            load_rows(w3_raw[0][a], w3, a, 0, 512)
        nc.sync.dma_start(out=w4_raw[:], in_=w4_words.bitcast(I32).rearrange("a p c -> p a c"))
        for q in range(4):
            nc.sync.dma_start(out=w4_sraw[32 * q:32 * q + 4, :].bitcast(I32).rearrange("r (a c) -> r a c", a=2),
                              in_=w4_scales[:, 4 * q:4 * q + 4, :].bitcast(I32).rearrange("a r c -> r a c"))
        nc.sync.dma_start(idx3[:], offs3)
        nc.sync.dma_start(out=wgo_sb[:], in_=wgo)

        def deal(copy, dst, src):
            copy(out=dst.rearrange("p (u t m) -> p u t m", t=4, m=P), in_=src.rearrange("p (u m t) -> p u t m", t=4, m=P))

        def w1_round(copy, b, raw, m0):
            n = raw.shape[2] // 4
            copy(out=w1_bf[b][:].rearrange("p (t m j) -> p m t j", t=4, j=4)[:, m0:m0 + n], in_=raw[:].rearrange("p j (m t) -> p m t j", t=4))

        def quantize(codes, scales, src):
            nc.vector.quantize_mx(out=codes.bitcast(E4M3), scales=scales, in_=src)

        for q in range(4):
            nc.vector.tensor_copy(out=w2_sraw[32 * q:32 * q + 4, :].bitcast(I32), in_=w2_rows[32 * q:32 * q + 4, :])
        deal(nc.vector.tensor_copy, w2_s[:], w2_sraw[:])
        nc.vector.tensor_copy(vs[:], tabs[:].indirect(idx1[:]))
        for half in range(2):
            nc.vector.tensor_copy(vw[:, half * BANK:(half + 1) * BANK], tabw[:].bitcast(U32).indirect(idx1[:, 32 * half:32 * (half + 1)]))
        deal(nc.scalar.copy, w2_c[:], w2_raw[:].bitcast(U16))
        w1_round(nc.scalar.copy, 0, w1_raw0[0], 0)
        w1_round(nc.vector.tensor_copy, 0, w1_raw0[1], 64)
        quantize(w1_c[0][:], w1_s[0][:], w1_bf[0][:])

        def features(s, half, mod_sb):
            b, i = divmod(s, 4)
            cols = slice(half * BANK, (half + 1) * BANK)
            mod = psum.tile([P, BANK], F32, name="left", tag="left")
            base = psum.tile([P, BANK], F32, name="right", tag="right")
            nc.tensor.matmul_mx(out=mod[:], lhsT=w2_c[:, s * P:(s + 1) * P].bitcast(E2M1), lhsT_scale=w2_s[:, s * P:(s + 1) * P],
                                rhs=vw[:, cols].bitcast(E4M3), rhs_scale=vs[:, cols], start=True, stop=True)
            nc.tensor.matmul_mx(out=base[:], lhsT=w1_c[b][:, i * P:(i + 1) * P].bitcast(E4M3), lhsT_scale=w1_s[b][:, i * P:(i + 1) * P],
                                rhs=vw[:, cols].bitcast(E4M3), rhs_scale=vs[:, cols], start=True, stop=True)
            nc.scalar.copy(out=mod_sb[:], in_=mod[:])
            nc.vector.scalar_tensor_tensor(out=hs[s][:, cols], in0=mod_sb[:], scalar=1.0, in1=base[:], op0=ALU.add, op1=ALU.mult)

        def pick(s, f, picked):
            b, i = divmod(s, 4)
            window = hs[s][:].indirect(idx2[:, 16 * f:16 * (f + 1)])
            weights = wgt_sb[:, f * MH:(f + 1) * MH]
            nc.vector.tensor_tensor(picked, window, weights, ALU.mult)
            nc.scalar.activation(out=x_pl[f][b][:, i, :], in_=picked, func=ACT.Identity, bias=bt_sb[:, b, i:i + 1])

        def x_quantize(copy, f, b):
            x_bf = ring.tile([P, 4 * MH], BF16, name="x_bf", align_bytes=64)
            copy(out=x_bf[:].rearrange("p (c e i) -> p c i e", e=4, i=4), in_=x_pl[f][b][:].rearrange("p i (c e) -> p c i e", e=4))
            quantize(x_c[b][:, f * MH:(f + 1) * MH], x_s[b][:, f * MH:(f + 1) * MH], x_bf[:])

        def w4_deal(b):
            words = w4_raw[:].bitcast(U16).rearrange("p a (b m t) -> p a b t m", b=2, t=4)[:, :, b]
            nc.scalar.copy(out=w4_c[:].rearrange("p (b a t m) -> p b a t m", b=2, a=2, t=4)[:, b], in_=words)
            nc.vector.tensor_copy(out=w4_s[:].rearrange("p (b a t m) -> p b a t m", b=2, a=2, t=4)[:, b],
                                  in_=w4_sraw[:].rearrange("p (a b m t) -> p a b t m", a=2, b=2, t=4)[:, :, b])

        def w3_prepare(u):
            b, pair = divmod(u, 2)
            w3_bf = ring.tile([P, 2, 1024], BF16, name="w3_bf", align_bytes=64, bufs=2)
            for a in range(2):
                nc.scalar.copy(out=w3_bf[:, a, :].rearrange("p (t m j) -> p m t j", t=2, j=4),
                               in_=w3_raw[b][a][:].rearrange("p j (m t) -> p m t j", t=4)[:, :, 2 * pair:2 * pair + 2, :])
            quantize(w3_c[u][:], w3_s[u][:], w3_bf[:].rearrange("p a c -> p (a c)"))

        for s in range(8):
            if s == 0:
                features(s, 0, held("mod_first", [P, BANK], F32, "first"))
            else:
                features(s, 0, ring.tile([P, BANK], F32, name="mod_sb"))
            if s > 0:
                pick(s - 1, 0, ring.tile([P, MH], F32, name="picked")[:])
            if s < 7:
                features(s, 1, ring.tile([P, BANK], F32, name="mod_sb"))
            else:
                features(s, 1, held("mod_last", [P, BANK], F32, "late"))
            if s == 0:
                w1_bf.append(held("w1_bf1", [P, 2048], BF16, "first"))
                w1_round(nc.scalar.copy, 1, w1_raw1, 0)
            if s == 2:
                quantize(w1_c[1][:], w1_s[1][:], w1_bf[1][:])
                w3_raw.append([held("w3_raw10", [P, 4, 512], F32, "raw_a"), held("w3_raw11", [P, 4, 512], F32, "tabw")])
                for a in range(2):
                    load_rows(w3_raw[1][a], w3, a, 512, 1024)
            if s == 3:
                w3_prepare(0)
            if s == 4:
                x_quantize(nc.scalar.copy, 0, 0)
            if s == 6:
                w4_deal(0)
        pick(7, 0, ring.tile([P, MH], F32, name="picked")[:])
        x_quantize(nc.scalar.copy, 0, 1)

        def grade(s, m0, m1):
            b, i = divmod(s, 4)
            u, t = divmod(s, 2)
            damp = psum.tile([P, m1 - m0], F32, name="left", tag="left")
            top = psum.tile([P, m1 - m0], F32, name="right", tag="right")
            for a in range(2):
                cols = slice((8 * b + 4 * a + i) * P, (8 * b + 4 * a + i + 1) * P)
                nc.tensor.matmul_mx(out=damp[:], lhsT=w4_c[:, cols].bitcast(E2M1), lhsT_scale=w4_s[:, cols],
                                    rhs=x_c[a][:, m0:m1].bitcast(E4M3), rhs_scale=x_s[a][:, m0:m1], start=(a == 0), stop=(a == 1))
            for a in range(2):
                cols = slice((2 * a + t) * P, (2 * a + t + 1) * P)
                nc.tensor.matmul_mx(out=top[:], lhsT=w3_c[u][:, cols].bitcast(E4M3), lhsT_scale=w3_s[u][:, cols],
                                    rhs=x_c[a][:, m0:m1].bitcast(E4M3), rhs_scale=x_s[a][:, m0:m1], start=(a == 0), stop=(a == 1))
            size = ring.tile([P, m1 - m0], F32, name="size")
            nc.scalar.activation(out=size[:], in_=damp[:], func=ACT.Abs)
            root = ring.tile([P, m1 - m0], F32, name="root")
            nc.scalar.activation(out=root[:], in_=size[:], func=ACT.Abs_reciprocal_sqrt, bias=1.0)
            inv = ring.tile([P, m1 - m0], F32, name="inv")
            nc.scalar.activation(out=inv[:], in_=root[:], func=ACT.Square)
            y = ring.tile([P, m1 - m0], F32, name="y")
            nc.vector.tensor_tensor(y[:], top[:], wgo_sb[:, m0:m1], ALU.mult)
            return y, inv

        def enter(s, m0, m1, y, inv):
            b, i = divmod(s, 4)
            nc.vector.tensor_tensor(pages[s % PAGES][:].indirect(idx3[:, m0 // 16:m1 // 16]), y[:], inv[:], ALU.mult)
            if m1 == M:
                nc.sync.dma_start(out=out[512 * b:512 * (b + 1), :].rearrange("(p i) c -> p i c", i=4)[:, i, :], in_=pages[s % PAGES][:])

        late = held("late", [P, 8, MH], F32, "late")
        units = [(s, 0, MH) for s in range(SPLIT)] + [(s, MH, M) for s in range(SPLIT)] + [(s, 0, M) for s in range(SPLIT, 8)]
        ys = [grade(*units[0])]
        for s in range(8):
            pick(s, 1, late[:, s, :])
            if s == 3:
                x_quantize(nc.scalar.copy, 1, 0)
        w3_prepare(1)
        x_quantize(nc.scalar.copy, 1, 1)
        for n in range(1, len(units)):
            ys.append(grade(*units[n]))
            if n == 2:
                w4_deal(1)
            if n == 3:
                w3_prepare(2)
            if n == 6:
                w3_prepare(3)
            enter(*units[n - 1], *ys[n - 1])
        enter(*units[-1], *ys[-1])
